import numpy as np
import ml_dtypes


def mxq(x, axis, fmt="e4m3"):
    dtype, down = {"e4m3": (ml_dtypes.float8_e4m3fn, 7), "e5m2": (ml_dtypes.float8_e5m2, 14)}[fmt]
    v = np.moveaxis(np.asarray(x, np.float32).astype(ml_dtypes.bfloat16).astype(np.float64), axis, -1)
    blocks = v.reshape(v.shape[:-1] + (-1, 32))
    amax = np.abs(blocks).max(-1, keepdims=True)
    byte = np.maximum(np.where(amax > 0, np.frexp(amax)[1] - 1 + 127, 0) - down, 1)
    scale = np.exp2(byte - 127.0)
    codes = (blocks / scale).astype(np.float32).astype(dtype).astype(np.float64)
    return np.moveaxis((codes * scale).reshape(v.shape), -1, axis)


WIDE = False


def mx_kscale(k):
    if not WIDE:
        return np.ones(k)
    levels = np.array([10, -10, 5, -5, 0])
    if k % 512:
        return np.exp2(np.random.permutation(np.resize(levels, k // 32))).repeat(32)
    a = np.empty((k // 512, 16))
    for p in range(k // 512):
        a[p, :8] = np.random.permutation(np.resize(levels, 8))
        for g in range(8):
            far = levels[np.abs(levels - a[p, g]) >= 10]
            a[p, g + 8] = far[np.random.randint(len(far))]
    return np.exp2(a.ravel()).repeat(32)


def f64(x):
    return np.asarray(x).astype(np.float64)


def striped(idx):
    return np.tile(idx.reshape(-1, 16).T, (8, 1)).astype(np.uint16)


def unstriped(offs):
    return offs[:16].T.reshape(-1).astype(np.int64)


E2M1 = np.array([0.0, 0.5, 1.0, 1.5, 2.0, 3.0, 4.0, 6.0, -0.0, -0.5, -1.0, -1.5, -2.0, -3.0, -4.0, -6.0])


def pack_weight(w, fmt):
    k, n = w.shape
    w = f64(np.asarray(w, np.float32).astype(ml_dtypes.bfloat16)).reshape(k // 32, 32, n)
    amax = np.abs(w).max(1)
    if fmt == "e4m3":
        byte = np.frexp(amax)[1] - 1 + 127 - 7
    else:
        mant, ex = np.frexp(amax / 6.0)
        byte = np.where(mant > 0.5, ex, ex - 1) + 127
    byte = np.clip(np.where(amax > 0, byte, 1), 1, 254)
    scaled = (w * np.exp2(127.0 - byte)[:, None, :]).reshape(k, n).astype(np.float32)
    by_word = np.ascontiguousarray(scaled.reshape(k // 512, 128, 4, n).transpose(0, 1, 3, 2))
    if fmt == "e4m3":
        words = by_word.astype(ml_dtypes.float8_e4m3fn).view(np.uint8)
    else:
        c = by_word.astype(ml_dtypes.float4_e2m1fn).view(np.uint8) & 0xF
        words = (c[..., 0::2] | (c[..., 1::2] << 4)).reshape(k // 512, 128, 2 * n)
    return np.ascontiguousarray(words), np.ascontiguousarray(byte.astype(np.uint8).reshape(k // 512, 16, n))


def unpack_weight(words, scales, fmt):
    g, _, n = scales.shape
    words = np.ascontiguousarray(words).reshape(g, 128, n, -1)
    if fmt == "e4m3":
        vals = words.view(ml_dtypes.float8_e4m3fn).astype(np.float64)
    else:
        nib = np.empty((g, 128, n, 4), np.uint8)
        nib[..., 0::2] = words & 0xF
        nib[..., 1::2] = words >> 4
        vals = E2M1[nib]
    vals = vals * np.repeat(np.exp2(scales.astype(np.float64) - 127.0), 8, axis=1)[..., None]
    return vals.transpose(0, 1, 3, 2).reshape(g * 512, n)


def gelu(v):
    return 0.5 * v * (1.0 + np.tanh(np.sqrt(2.0 / np.pi) * (v + 0.044715 * v**3)))


def bf(x):
    return np.asarray(x, np.float32).astype(ml_dtypes.bfloat16)


def planes(Y):
    n, m = Y.shape
    b = f64(bf(Y)).reshape(n // 32, 32, m)
    amax = np.abs(b).max(1)
    byte = np.clip(np.where(amax > 0, np.frexp(amax)[1] - 1 + 127 - 7, 1), 1, 254)
    codes = (b * np.exp2(127.0 - byte)[:, None, :]).reshape(n, m).astype(np.float32).astype(ml_dtypes.float8_e4m3fn).view(np.uint8)
    words = codes.reshape(n // 512, 128, 4, m).transpose(0, 1, 3, 2)
    return np.ascontiguousarray(words), np.ascontiguousarray(byte.astype(np.uint8).reshape(n // 512, 16, m))


K, M, H, N, T, S = 1024, 512, 1024, 512, 4096, 1024

def setup_inputs():
    n = np.random.standard_normal
    s, um, u = mx_kscale(K)[:, None], mx_kscale(M)[:, None], mx_kscale(H)[:, None]
    d = {}
    d["tab_words"], d["tab_scales"] = pack_weight(n((K, T)) * s, "e4m3")
    d["offs"] = striped(np.random.permutation(T)[:S])
    d["xs_words"], d["xs_scales"] = pack_weight(n((K, S)) * s, "e4m3")
    d["w1"] = (1.5 * n((K, M)) / s / K**0.5).astype(np.float32)
    d["shift"] = (0.5 * n(M)).astype(np.float32)
    d["gain"] = (np.exp(0.3 * n(M)) * um[:, 0]).astype(np.float32)
    d["w2_words"], d["w2_scales"] = pack_weight(1.2 * n((M, H)) / um * u.T / M**0.5, "e2m1")
    d["w3"] = (n((K, H)) / s * u.T / K**0.5).astype(np.float32)
    d["w4"] = (n((H, N)) / u * np.exp(0.8 * n(N))[None, :] / H**0.5).astype(np.float32)
    return d

def reference(tab_words, tab_scales, offs, xs_words, xs_scales, w1, shift, gain, w2_words, w2_scales, w3, w4):
    v = unpack_weight(tab_words, tab_scales, "e4m3")[:, unstriped(offs)]
    xs = unpack_weight(xs_words, xs_scales, "e4m3")
    w2 = unpack_weight(w2_words, w2_scales, "e2m1")
    sky = mxq(f64(w1), 0, "e4m3").T @ xs
    t = f64(gain)[:, None] * (np.tanh(sky) - f64(shift)[:, None])
    b = w2.T @ mxq(t, 0, "e4m3")
    a = mxq(f64(w3), 0, "e4m3").T @ v
    z = np.minimum(a, b) + a
    y = mxq(f64(w4), 0, "e4m3").T @ mxq(z, 0, "e4m3")
    words, scales = planes(y)
    return y, words, scales

from contextlib import ExitStack

import concourse.mybir as mybir

K, M, H, N, T, S = 1024, 512, 1024, 512, 4096, 1024
FLOPS = 2 * S * (K * M + M * H + K * H + H * N)

F32 = mybir.dt.float32
BF16 = mybir.dt.bfloat16
I32 = mybir.dt.int32
U32 = mybir.dt.uint32
U16 = mybir.dt.uint16
U8 = mybir.dt.uint8
E4M3 = mybir.dt.float8_e4m3fn_x4
E2M1 = mybir.dt.float4_e2m1fn_x4
ALU = mybir.AluOpType
TANH = mybir.ActivationFunctionType.Tanh

P = 128
PACK = 4
PASS = P * PACK
HALF = 512
UNIT = 128
Y_WIDTHS = (256, 256, 256, 128, 128)
TWICE_EVERY = 4
STAGES = 6
BANKS = {"copied": (0, 1), "read_twice": (2, 3, 4), "y": (5, 6, 7)}


def tile_list_heliostat_aim_features_kernel(
    tc, tab_words, tab_scales, offs, xs_words, xs_scales, w1, shift, gain, w2_words, w2_scales, w3, w4,
    out_0, out_1, out_2,
):
    nc = tc.nc
    with ExitStack() as ctx:
        lists = ctx.enter_context(tc.tile_pool(name="lists", bufs=1))
        keep = ctx.enter_context(tc.tile_pool(name="keep", bufs=1))
        ring = ctx.enter_context(tc.tile_pool(name="ring", bufs=2))
        psum = ctx.enter_context(tc.psum_pool(name="psum", bufs=1))

        turns = {"copied": 0, "read_twice": 0, "y": 0}

        def take_bank(role, shape):
            banks = BANKS[role]
            turns[role] = turns[role] + 1
            return psum.tile(shape, F32, name=role, tag="bank_%d" % banks[turns[role] % len(banks)])

        def kept(shape, dtype, name):
            return keep.tile(shape, dtype, name=name, align_bytes=64)

        def words_view(words):
            return words.rearrange("p c i -> p (c i)").bitcast(I32)

        def load_planes(queue, plane, scales, quadrants, first_row=0):
            passes = scales.shape[0]
            for q in quadrants:
                queue.dma_start(
                    out=plane[32 * q + first_row : 32 * q + first_row + 4 * passes, :].bitcast(I32),
                    in_=scales[:, 4 * q : 4 * q + 4, :].bitcast(I32),
                )

        def load_rows(rows):
            raw = ring.tile([P, PACK, PASS], F32, name="raw", bufs=4)
            nc.sync.dma_start(out=raw[:], in_=rows.rearrange("(p j) c -> p j c", j=PACK))
            return raw

        def copy_on(engine, out, in_):
            if engine == "vector":
                nc.vector.tensor_copy(out=out, in_=in_)
            else:
                half = out.shape[1] // 2
                for part in (slice(0, half), slice(half, 2 * half)):
                    nc.scalar.copy(out=out[:, part], in_=in_[:, part])

        def round_dealt_by_ones(raw, engine, slot):
            grouped = keep.tile([P, PACK * PASS], BF16, name="grouped", tag=slot, align_bytes=64)
            copy_on(
                engine,
                grouped[:].rearrange("p (t m j) -> p m j t", t=PACK, j=PACK),
                raw[:].rearrange("p j (m t) -> p m j t", t=PACK),
            )
            return grouped

        def round_dealt_by_fours(raw, engine, slot):
            grouped = keep.tile([P, PACK * PASS], BF16, name="grouped", tag=slot, align_bytes=64)
            copy_on(
                engine,
                grouped[:].rearrange("p (t u i j) -> p u t j i", t=PACK, i=4, j=PACK),
                raw[:].rearrange("p j (u t i) -> p u t j i", t=PACK, i=4),
            )
            return grouped

        def quantise(grouped, width, name):
            codes = kept([P, width], U32, name + "_codes")
            scales = kept([P, width], U8, name + "_scales")
            nc.vector.quantize_mx(out=codes[:].bitcast(E4M3), scales=scales[:], in_=grouped)
            return codes, scales

        def interleave(engine, out, in_):
            copy_on(
                engine,
                out.rearrange("p (c i t) -> p c t i", i=4, t=PACK),
                in_.rearrange("p t (c i) -> p c t i", i=4),
            )

        xs_plane = kept([P, S], U8, "xs_plane")
        w2_plane = kept([P, H], U8, "w2_plane")
        tab_plane = kept([P, T], U8, "tab_plane")
        nc.vector.memset(tab_plane[:, 0 : T // 2].bitcast(I32), 0)
        nc.gpsimd.memset(tab_plane[:, T // 2 : T].bitcast(I32), 0)
        nc.vector.memset(w2_plane[:].bitcast(I32), 0)
        load_planes(nc.scalar, xs_plane, xs_scales, range(4), 4)
        w1_raw = [load_rows(w1[a * PASS : (a + 1) * PASS, :]) for a in range(2)]
        xs_sb = [kept([P, 2, HALF], U32, "xs_%d" % h) for h in range(2)]

        def load_xs(h):
            nc.sync.dma_start(
                out=xs_sb[h][:].bitcast(I32),
                in_=xs_words[:, :, h * HALF : (h + 1) * HALF, :].rearrange("a p c i -> p a (c i)").bitcast(I32),
            )

        load_xs(0)
        offsets = lists.tile([P, S // 16], U16, name="offsets")
        nc.sync.dma_start(offsets[:], offs)
        load_planes(nc.sync, tab_plane, tab_scales, range(4))
        load_xs(1)
        shift_sb = kept([P, PACK], F32, "shift_sb")
        gain_sb = kept([P, PACK], F32, "gain_sb")
        nc.sync.dma_start(out=shift_sb[:], in_=shift.rearrange("(p t) -> p t", t=PACK))
        nc.sync.dma_start(out=gain_sb[:], in_=gain.rearrange("(p t) -> p t", t=PACK))
        w2_sb = kept([P, 2 * H], U8, "w2_sb")
        nc.sync.dma_start(out=w2_sb[:].bitcast(I32), in_=w2_words[0].bitcast(I32))
        w3_raw = {}
        w3_raw[0, 0] = load_rows(w3[0:PASS, 0:PASS])
        load_planes(nc.sync, w2_plane, w2_scales, (0, 1))
        w3_raw[0, 1] = load_rows(w3[PASS : 2 * PASS, 0:PASS])
        load_planes(nc.sync, w2_plane, w2_scales, (2, 3))
        tab_sb = [kept([P, T], U32, "tab_%d" % a) for a in range(2)]
        nc.sync.dma_start(out=tab_sb[0][:].bitcast(I32), in_=words_view(tab_words[0]))
        nc.sync.dma_start(out=tab_sb[1][:].bitcast(I32), in_=words_view(tab_words[1]))

        w1_q = []
        for a, engine in ((0, "scalar"), (1, "vector")):
            grouped = round_dealt_by_ones(w1_raw[a], engine, "rows_%d" % a)
            codes = kept([P, M], U32, "w1_codes_%d" % a)
            scales = xs_plane[:, a * M : (a + 1) * M]
            nc.vector.quantize_mx(out=codes[:].bitcast(E4M3), scales=scales, in_=grouped[:])
            w1_q.append((codes, scales))

        for a in range(2):
            w3_raw[1, a] = load_rows(w3[a * PASS : (a + 1) * PASS, PASS : 2 * PASS])

        v_plane = kept([P, S], U8, "v_plane")
        nc.vector.tensor_copy(out=v_plane[:], in_=tab_plane[:].indirect(offsets[:]))

        def deal_w2():
            w2_dealt = keep.tile([P, 2 * H], U8, name="w2_dealt", tag="bounded_0", align_bytes=64)
            w2_plane_dealt = keep.tile([P, H], U8, name="w2_plane_dealt", tag="bounded_1", align_bytes=64)
            nc.vector.tensor_copy(
                out=w2_dealt[:].bitcast(I32).rearrange("p (g t u e) -> p g t u e", g=2, t=PACK, e=2),
                in_=w2_sb[:].bitcast(I32).rearrange("p (g u t e) -> p g t u e", g=2, t=PACK, e=2),
            )
            nc.vector.tensor_copy(
                out=w2_plane_dealt[:].bitcast(I32).rearrange("p (g t u) -> p g t u", g=2, t=PACK),
                in_=w2_plane[:].bitcast(I32).rearrange("p (g u t) -> p g t u", g=2, t=PACK),
            )
            return w2_dealt, w2_plane_dealt

        t_q = []
        w3_q = {}
        for h in range(2):
            t_rows = keep.tile([P, PACK, HALF], BF16, name="t_rows", tag="rows_%d" % h, align_bytes=64)
            sky = [psum.tile([P, HALF], F32, name="sky", tag="bank_%d" % (PACK * h + t)) for t in range(PACK)]
            for t in range(PACK):
                for a in range(2):
                    codes, scales = w1_q[a]
                    nc.tensor.matmul_mx(
                        out=sky[t][:],
                        lhsT=codes[:, t * P : (t + 1) * P].bitcast(E4M3),
                        lhsT_scale=scales[:, t * P : (t + 1) * P],
                        rhs=xs_sb[h][:, a, :].bitcast(E4M3),
                        rhs_scale=xs_plane[4 + 4 * a : P, h * HALF : (h + 1) * HALF],
                        start=(a == 0),
                        stop=(a == 1),
                    )
            for t in range(PACK):
                bounded = keep.tile([P, HALF], F32, name="bounded", tag="bounded_%d" % ((PACK * h + t) % 3), align_bytes=64)
                nc.scalar.activation(out=bounded[:], in_=sky[t][:], func=TANH)
                nc.vector.tensor_scalar(
                    out=t_rows[:, t, :], in0=bounded[:], scalar1=shift_sb[:, t : t + 1], scalar2=gain_sb[:, t : t + 1],
                    op0=ALU.subtract, op1=ALU.mult,
                )
            if h == 1:
                w2_dealt, w2_plane_dealt = deal_w2()
            t_grouped = keep.tile([P, PACK * HALF], BF16, name="t_grouped", tag="words_%d" % h, align_bytes=64)
            interleave("vector", t_grouped[:], t_rows[:])
            t_q.append(quantise(t_grouped[:], HALF, "t_%d" % h))

        for a, engine in ((0, "scalar"), (1, "scalar")):
            w3_q[0, a] = quantise(round_dealt_by_fours(w3_raw[0, a], engine, "rows_%d" % a)[:], PASS, "w3_0%d" % a)

        w4_raw = []
        for g in range(2):
            raw = ring.tile([P, PACK, PASS], F32, name="raw", bufs=4)
            rows = w4[g * PASS : (g + 1) * PASS, :].rearrange("(u t i) c -> t u i c", t=PACK, i=4)
            for t in range(PACK):
                nc.sync.dma_start(out=raw[:, t, :], in_=rows[t])
            w4_raw.append(raw)

        v_words = {}

        def gather(a, h):
            slot = "words_%d" % (1 - h) if a == 0 else "v_%d%d" % (a, h)
            picked = keep.tile([P, HALF], U32, name="picked", tag=slot, align_bytes=64)
            cols = HALF // 16
            nc.vector.tensor_copy(out=picked[:], in_=tab_sb[a][:].indirect(offsets[:, h * cols : (h + 1) * cols]))
            v_words[a, h] = picked

        units = [(g, jb) for g in range(2) for jb in range(S // UNIT)]
        b_sb, slot_of, late = {}, {}, {}

        def b_pass(out, g, t, jb, start):
            h, c0 = divmod(jb * UNIT, HALF)
            codes, scales = t_q[h]
            r0 = g * PASS + t * P
            nc.tensor.matmul_mx(
                out=out,
                lhsT=w2_dealt[:, 2 * r0 : 2 * (r0 + P)].bitcast(E2M1),
                lhsT_scale=w2_plane_dealt[:, r0 : r0 + P],
                rhs=codes[:, c0 : c0 + UNIT].bitcast(E4M3),
                rhs_scale=scales[:, c0 : c0 + UNIT],
                start=start,
                stop=True,
            )

        def a_passes(out, g, t, jb, stop):
            h, c0 = divmod(jb * UNIT, HALF)
            for a in range(2):
                codes, scales = w3_q[g, a]
                nc.tensor.matmul_mx(
                    out=out,
                    lhsT=codes[:, t * P : (t + 1) * P].bitcast(E4M3),
                    lhsT_scale=scales[:, t * P : (t + 1) * P],
                    rhs=v_words[a, h][:, c0 : c0 + UNIT].bitcast(E4M3),
                    rhs_scale=v_plane[4 * a : P, jb * UNIT : (jb + 1) * UNIT],
                    start=(a == 0),
                    stop=(stop and a == 1),
                )

        def make_b(g, jb, slot):
            bank = take_bank("copied", [P, PACK, UNIT])
            for t in range(PACK):
                b_pass(bank[:, t, :], g, t, jb, True)
            b_tile = keep.tile([P, UNIT, PACK], F32, name="b_tile", tag=slot, align_bytes=64)
            nc.scalar.copy(out=b_tile[:], in_=bank[:].rearrange("p t j -> p j t"))
            b_sb[g, jb] = b_tile
            slot_of["b", g, jb] = slot

        twice = units[TWICE_EVERY - 1 :: TWICE_EVERY]
        once = [u for u in units if u not in twice]
        for k, u in enumerate(once[:STAGES]):
            make_b(*u, "stage_%d" % k)
        b_later = [("b", *u) for u in once[STAGES:]]
        waiting = [("w3", 0), b_later[0], ("w3", 1), ("w4", 0), *b_later[1:3], ("w4", 1), *b_later[3:]]

        def pass_slot_on(tenant):
            slot = slot_of[tenant]
            if waiting:
                item = waiting[0]
                waiting.remove(item)
                if item[0] == "b":
                    make_b(*item[1:], slot)
                elif item[0] == "w3":
                    late[item] = round_dealt_by_fours(w3_raw[1, item[1]], "scalar", slot)
                else:
                    late[item] = round_dealt_by_ones(w4_raw[item[1]], "scalar", slot)
                slot_of[item] = slot

        gather(0, 0)
        gather(0, 1)
        gather(1, 0)

        a_banks, lesser = {}, {}

        def take_min(g, jb):
            bank = take_bank("read_twice", [P, PACK, UNIT])
            for t in range(PACK):
                a_passes(bank[:, t, :], g, t, jb, True)
            low = ring.tile([P, UNIT, PACK], F32, name="low", bufs=3)
            nc.vector.tensor_tensor(out=low[:], in0=bank[:].rearrange("p t j -> p j t"), in1=b_sb[g, jb][:], op=ALU.min)
            a_banks[g, jb], lesser[g, jb] = bank, low
            pass_slot_on(("b", g, jb))

        def double_a(g, jb):
            bank = take_bank("copied", [P, PACK, UNIT])
            for t in range(PACK):
                a_passes(bank[:, t, :], g, t, jb, True)
            low = ring.tile([P, UNIT, PACK], F32, name="low", bufs=3)
            nc.scalar.mul(out=low[:], in_=bank[:].rearrange("p t j -> p j t"), mul=2.0)
            both = take_bank("read_twice", [P, PACK, UNIT])
            for t in range(PACK):
                a_passes(both[:, t, :], g, t, jb, False)
                b_pass(both[:, t, :], g, t, jb, False)
            a_banks[g, jb], lesser[g, jb] = both, low

        blocks = []
        j0 = 0
        for width in Y_WIDTHS:
            blocks.append((j0, width))
            j0 = j0 + width
        block_of = {jb: b for b, (j0, width) in enumerate(blocks) for jb in range(j0 // UNIT, (j0 + width) // UNIT)}
        z_tiles, z_q = {}, {}

        def add_a(g, jb, op):
            b = block_of[jb]
            j0, width = blocks[b]
            if (g, b) not in z_tiles:
                z_tiles[g, b] = ring.tile([P, width, PACK], BF16, name="z_tile", bufs=3, align_bytes=64)
            c0 = jb * UNIT - j0
            nc.vector.tensor_tensor(
                out=z_tiles[g, b][:, c0 : c0 + UNIT, :],
                in0=a_banks[g, jb][:].rearrange("p t j -> p j t"), in1=lesser[g, jb][:], op=op,
            )

        y_plane = kept([P, S], U8, "y_plane")
        w4_q = []
        out_rows = out_0.rearrange("(p t) j -> p t j", t=PACK)

        def finish(b):
            j0, width = blocks[b]
            y_rows = ring.tile([P, PACK, width], F32, name="y_rows", bufs=3)
            per_bank = HALF // width
            for t0 in range(0, PACK, per_bank):
                bank = take_bank("y", [P, per_bank, width])
                for t in range(t0, t0 + per_bank):
                    for g in range(2):
                        codes, scales = w4_q[g]
                        z_codes, z_scales = z_q[g, b]
                        nc.tensor.matmul_mx(
                            out=bank[:, t - t0, :],
                            lhsT=codes[:, t * P : (t + 1) * P].bitcast(E4M3),
                            lhsT_scale=scales[:, t * P : (t + 1) * P],
                            rhs=z_codes[:].bitcast(E4M3),
                            rhs_scale=z_scales[:],
                            start=(g == 0),
                            stop=(g == 1),
                        )
                nc.scalar.copy(out=y_rows[:, t0 : t0 + per_bank, :], in_=bank[:])
            nc.sync.dma_start(out=out_rows[:, :, j0 : j0 + width], in_=y_rows[:])
            y_grouped = ring.tile([P, PACK * width], BF16, name="y_grouped", bufs=2, align_bytes=64)
            interleave("vector" if b == len(blocks) - 1 else "scalar", y_grouped[:], y_rows[:])
            return y_grouped

        def finish_planes(b, y_grouped):
            j0, width = blocks[b]
            y_codes = kept([P, width], U32, "y_codes_%d" % b)
            nc.vector.quantize_mx(out=y_codes[:].bitcast(E4M3), scales=y_plane[:, j0 : j0 + width], in_=y_grouped[:])
            nc.sync.dma_start(out=words_view(out_1[0, :, j0 : j0 + width, :]), in_=y_codes[:].bitcast(I32))

        def block_done(g, jb):
            return jb + 1 == S // UNIT or block_of[jb + 1] != block_of[jb]

        pending = []
        for n in range(len(units) + 2):
            if n < len(units):
                if units[n] in twice:
                    double_a(*units[n])
                else:
                    take_min(*units[n])
            if n == 1:
                gather(1, 1)
            if n >= 2 and block_done(*units[n - 2]):
                g, jb = units[n - 2]
                b = block_of[jb]
                z_q[g, b] = quantise(
                    z_tiles[g, b][:].rearrange("p j t -> p (j t)"), blocks[b][1], "z_%d%d" % (g, b)
                )
                if g == 1:
                    for done in pending:
                        finish_planes(*done)
                    pending = [(b, finish(b))]
            if 1 <= n <= len(units):
                add_a(*units[n - 1], ALU.min if units[n - 1] in twice else ALU.add)
            if n in (5, 6):
                w3_q[1, n - 5] = quantise(late["w3", n - 5][:], PASS, "w3_1%d" % (n - 5))
                pass_slot_on(("w3", n - 5))
            if n in (8, 9):
                w4_q.append(quantise(late["w4", n - 8][:], N, "w4_%d" % (n - 8)))
                pass_slot_on(("w4", n - 8))
        for done in pending:
            finish_planes(*done)
        for q in range(4):
            queue = nc.sync if q % 2 == 0 else nc.scalar
            queue.dma_start(
                out=out_2[0, 4 * q : 4 * q + 4, :].bitcast(I32), in_=y_plane[32 * q : 32 * q + 4, :].bitcast(I32)
            )
